import numpy as np
import ml_dtypes


def mxq(x, axis, fmt="e4m3"):
    dtype, down = {"e4m3": (ml_dtypes.float8_e4m3fn, 7), "e5m2": (ml_dtypes.float8_e5m2, 14)}[fmt]
    v = np.moveaxis(np.asarray(x, np.float32).astype(ml_dtypes.bfloat16).astype(np.float64), axis, -1)
    blocks = v.reshape(v.shape[:-1] + (-1, 32))
    amax = np.abs(blocks).max(-1, keepdims=True)
    byte = np.maximum(np.where(amax > 0, np.frexp(amax)[1] - 1 + 127, 0) - down, 1)
    scale = np.exp2(byte - 127.0)
    codes = (blocks / scale).astype(np.float32).astype(dtype).astype(np.float64)
    return np.moveaxis((codes * scale).reshape(v.shape), -1, axis)


WIDE = False


def mx_kscale(k):
    if not WIDE:
        return np.ones(k)
    levels = np.array([10, -10, 5, -5, 0])
    if k % 512:
        return np.exp2(np.random.permutation(np.resize(levels, k // 32))).repeat(32)
    a = np.empty((k // 512, 16))
    for p in range(k // 512):
        a[p, :8] = np.random.permutation(np.resize(levels, 8))
        for g in range(8):
            far = levels[np.abs(levels - a[p, g]) >= 10]
            a[p, g + 8] = far[np.random.randint(len(far))]
    return np.exp2(a.ravel()).repeat(32)


def f64(x):
    return np.asarray(x).astype(np.float64)


E2M1 = np.array([0.0, 0.5, 1.0, 1.5, 2.0, 3.0, 4.0, 6.0, -0.0, -0.5, -1.0, -1.5, -2.0, -3.0, -4.0, -6.0])


def pack_weight(w, fmt):
    k, n = w.shape
    w = f64(np.asarray(w, np.float32).astype(ml_dtypes.bfloat16)).reshape(k // 32, 32, n)
    amax = np.abs(w).max(1)
    if fmt == "e4m3":
        byte = np.frexp(amax)[1] - 1 + 127 - 7
    else:
        mant, ex = np.frexp(amax / 6.0)
        byte = np.where(mant > 0.5, ex, ex - 1) + 127
    byte = np.clip(np.where(amax > 0, byte, 1), 1, 254)
    scaled = (w * np.exp2(127.0 - byte)[:, None, :]).reshape(k, n).astype(np.float32)
    by_word = np.ascontiguousarray(scaled.reshape(k // 512, 128, 4, n).transpose(0, 1, 3, 2))
    if fmt == "e4m3":
        words = by_word.astype(ml_dtypes.float8_e4m3fn).view(np.uint8)
    else:
        c = by_word.astype(ml_dtypes.float4_e2m1fn).view(np.uint8) & 0xF
        words = (c[..., 0::2] | (c[..., 1::2] << 4)).reshape(k // 512, 128, 2 * n)
    return np.ascontiguousarray(words), np.ascontiguousarray(byte.astype(np.uint8).reshape(k // 512, 16, n))


def unpack_weight(words, scales, fmt):
    g, _, n = scales.shape
    words = np.ascontiguousarray(words).reshape(g, 128, n, -1)
    if fmt == "e4m3":
        vals = words.view(ml_dtypes.float8_e4m3fn).astype(np.float64)
    else:
        nib = np.empty((g, 128, n, 4), np.uint8)
        nib[..., 0::2] = words & 0xF
        nib[..., 1::2] = words >> 4
        vals = E2M1[nib]
    vals = vals * np.repeat(np.exp2(scales.astype(np.float64) - 127.0), 8, axis=1)[..., None]
    return vals.transpose(0, 1, 3, 2).reshape(g * 512, n)


def bf(x):
    return np.asarray(x, np.float32).astype(ml_dtypes.bfloat16)


def planes(Y):
    r, m = Y.shape
    b = f64(bf(Y)).reshape(r // 32, 32, m)
    amax = np.abs(b).max(1)
    byte = np.clip(np.where(amax > 0, np.frexp(amax)[1] - 1 + 127 - 7, 1), 1, 254)
    codes = (b * np.exp2(127.0 - byte)[:, None, :]).reshape(r, m).astype(np.float32).astype(ml_dtypes.float8_e4m3fn).view(np.uint8)
    words = codes.reshape(r // 512, 128, 4, m).transpose(0, 1, 3, 2)
    return np.ascontiguousarray(words), np.ascontiguousarray(byte.astype(np.uint8).reshape(r // 512, 16, m))


K, L, T, B, N = 512, 1024, 1024, 512, 512


def setup_inputs():
    n = np.random.standard_normal
    fk = mx_kscale(K)
    fl = mx_kscale(L)
    wap = pack_weight(n((K, N)) * 1 / np.sqrt(K) * fk[:, None], "e4m3")
    wbp = pack_weight(n((K, N)) * 1 / np.sqrt(K) * fk[:, None], "e2m1")
    xqp = pack_weight(n((L, T)) / fl[:, None], "e4m3")
    wqp = pack_weight(n((L, N)) * 1 / np.sqrt(L) * fl[:, None], "e2m1")
    return {
        "xf": (n((K, T))).astype(np.float32),
        "fa": (np.random.uniform(0.5, 2.0, (K, 1)) / fk[:, None]).astype(np.float32),
        "fb": (np.random.uniform(0.5, 2.0, (K, 1)) / fk[:, None]).astype(np.float32),
        "wa_words": wap[0],
        "wa_scales": wap[1],
        "wb_words": wbp[0],
        "wb_scales": wbp[1],
        "xq_words": xqp[0],
        "xq_scales": xqp[1],
        "wq_words": wqp[0],
        "wq_scales": wqp[1],
    }


def reference(xf, fa, fb, wa_words, wa_scales, wb_words, wb_scales, xq_words, xq_scales, wq_words, wq_scales):
    wau = unpack_weight(wa_words, wa_scales, "e4m3")
    wbu = unpack_weight(wb_words, wb_scales, "e2m1")
    xqu = unpack_weight(xq_words, xq_scales, "e4m3")
    wqu = unpack_weight(wq_words, wq_scales, "e2m1")
    m = f64(xf).reshape(K, B, T // B).max(axis=2)
    u = m * f64(fa)
    mr = np.repeat(m, T // B, axis=1)
    d = (mr - f64(xf)) * f64(fb)
    uq = mxq(u, 0, "e4m3")
    za = wau.T @ uq
    ra = np.maximum(za, 0.0)
    zr = np.repeat(ra, T // B, axis=1)
    dq = mxq(d, 0, "e4m3")
    zb = wbu.T @ dq + wqu.T @ xqu
    y = zr + zb
    words, scales = planes(y)
    return y, words, scales

@@ -1,0 +1,290 @@
+from contextlib import ExitStack
+
+import concourse.mybir as mybir
+
+K, L, T, B, N = 512, 1024, 1024, 512, 512
+FLOPS = 2 * N * (K * B + K * T + L * T)
+
+F32 = mybir.dt.float32
+BF16 = mybir.dt.bfloat16
+I32 = mybir.dt.int32
+U32 = mybir.dt.uint32
+U8 = mybir.dt.uint8
+FP8X4 = mybir.dt.float8_e4m3fn_x4
+FP4X4 = mybir.dt.float4_e2m1fn_x4
+ALU = mybir.AluOpType
+ACT = mybir.ActivationFunctionType
+
+P = 128
+PACK = 4
+PASSES_L = L // (P * PACK)
+CHUNK = 256
+PAIRS = CHUNK // 2
+CHUNKS = T // CHUNK
+BLOCK = 128
+HALF = 512
+ZB_BANKS = 6
+ZA_BANKS = 2
+
+
+def tile_mix_group_peak_and_members_pl_kernel(
+    tc, xf, fa, fb, wa_words, wa_scales, wb_words, wb_scales, xq_words, xq_scales, wq_words, wq_scales,
+    out_0, out_1, out_2,
+):
+    nc = tc.nc
+    with ExitStack() as ctx:
+        sb = ctx.enter_context(tc.tile_pool(name="sb", bufs=1))
+        zb_pool = ctx.enter_context(tc.psum_pool(name="zb", bufs=ZB_BANKS))
+        za_pool = ctx.enter_context(tc.psum_pool(name="za", bufs=ZA_BANKS))
+        ctx.enter_context(tc.manual_schedule())
+
+        def tiles(name, count, shape, dtype):
+            return [sb.tile(shape, dtype, name="%s%d" % (name, i), align_bytes=64) for i in range(count)]
+
+        def one(name, shape, dtype):
+            return sb.tile(shape, dtype, name=name, align_bytes=64)
+
+        x = tiles("x", CHUNKS, [P, PACK, CHUNK], F32)
+        peak = tiles("peak", CHUNKS, [P, PACK, PAIRS], F32)
+        diff = tiles("diff", CHUNKS, [P, PACK, PAIRS], F32)
+        u_rows = tiles("u_rows", CHUNKS, [P, PACK, PAIRS], BF16)
+        d_rows = tiles("d_rows", CHUNKS, [P, 2 * PACK, PAIRS], BF16)
+        u_in = tiles("u_in", CHUNKS, [P, PAIRS * PACK], BF16)
+        d_in = tiles("d_in", CHUNKS, [P, CHUNK * PACK], BF16)
+        u_codes = tiles("u_codes", CHUNKS, [P, PAIRS], U32)
+        u_plane = tiles("u_plane", CHUNKS, [P, PAIRS], U8)
+        d_codes = tiles("d_codes", CHUNKS, [P, CHUNK], U32)
+        d_plane = tiles("d_plane", CHUNKS, [P, CHUNK], U8)
+        ra = tiles("ra", CHUNKS, [P, PACK, PAIRS], F32)
+        y = tiles("y", CHUNKS, [P, PACK, CHUNK], F32)
+        y_in = tiles("y_in", CHUNKS, [P, CHUNK * PACK], BF16)
+        xq = tiles("xq", T // HALF, [P, PASSES_L, HALF], U32)
+        fa_sb = one("fa_sb", [P, PACK], F32)
+        fb_sb = one("fb_sb", [P, PACK], F32)
+        fb_neg = one("fb_neg", [P, PACK], F32)
+        wa_raw = one("wa_raw", [P, N], U32)
+        wa = one("wa", [P, N], U32)
+        wb_raw = one("wb_raw", [P, 2 * N], U8)
+        wb = one("wb", [P, 2 * N], U8)
+        wq_raw = one("wq_raw", [P, PASSES_L * 2 * N], U8)
+        wq = one("wq", [P, PASSES_L * 2 * N], U8)
+        ab_plane_raw = one("ab_plane_raw", [P, N], U8)
+        ab_plane = one("ab_plane", [P, N], U8)
+        wq_plane_raw = one("wq_plane_raw", [P, PASSES_L * N], U8)
+        wq_plane = one("wq_plane", [P, PASSES_L * N], U8)
+        xq_plane = one("xq_plane", [P, PASSES_L * T], U8)
+        y_codes = one("y_codes", [P, T], U32)
+        y_plane = one("y_plane", [P, T], U8)
+
+        xf_rows = xf.rearrange("(p j) t -> p j t", j=PACK)
+        out_rows = out_0.rearrange("(p r) t -> p r t", r=PACK)
+        out_words = out_1[0].rearrange("p t r -> p (t r)").bitcast(I32)
+
+        def load_x(c):
+            nc.sync.dma_start(out=x[c][:], in_=xf_rows[:, :, c * CHUNK:(c + 1) * CHUNK])
+
+        def load_xq(h):
+            src = xq_words.rearrange("z p t r -> p z (t r)")[:, :, h * HALF * 4:(h + 1) * HALF * 4]
+            nc.sync.dma_start(out=xq[h][:].bitcast(I32), in_=src.bitcast(I32))
+
+        def load_scales(queue, plane, first, scales):
+            rows = scales.bitcast(I32).rearrange("z (q r) c -> r q z c", r=4)
+            words = plane[:].bitcast(I32).rearrange("p (z c) -> p z c", z=scales.shape[0])
+            for r in range(4):
+                queue.dma_start(out=words[first + r:P:32, :, :], in_=rows[r])
+
+        nc.vector.memset(wq_plane_raw[:].bitcast(I32), 0)
+        nc.vector.memset(ab_plane_raw[:].bitcast(I32), 0)
+        nc.gpsimd.memset(xq_plane[:].bitcast(I32), 0)
+
+        load_scales(nc.gpsimd, xq_plane, 0, xq_scales)
+        nc.sync.dma_start(out=wq_raw[:].bitcast(I32).rearrange("p (z c) -> p z c", z=PASSES_L), in_=wq_words.rearrange("z p c -> p z c").bitcast(I32))
+        load_x(0)
+        nc.sync.dma_start(out=fa_sb[:], in_=fa.rearrange("(p j) o -> p (j o)", j=PACK))
+        nc.sync.dma_start(out=fb_sb[:], in_=fb.rearrange("(p j) o -> p (j o)", j=PACK))
+        load_x(1)
+        load_scales(nc.sync, wq_plane_raw, 0, wq_scales)
+        load_xq(0)
+        load_x(2)
+        nc.sync.dma_start(out=wb_raw[:].bitcast(I32), in_=wb_words[0].bitcast(I32))
+        nc.sync.dma_start(out=wa_raw[:].bitcast(I32), in_=wa_words[0].rearrange("p n r -> p (n r)").bitcast(I32))
+        load_x(3)
+        load_scales(nc.sync, ab_plane_raw, 0, wb_scales)
+        load_scales(nc.sync, ab_plane_raw, 4, wa_scales)
+        load_xq(1)
+
+        nc.scalar.activation(out=fb_neg[:], in_=fb_sb[:], func=ACT.Copy, scale=-1.0)
+
+        def pair_stats(c):
+            xs = x[c][:].rearrange("p j (b s) -> p (j b) s", s=2)
+            flat = "p j b -> p (j b)"
+            nc.vector.tensor_tensor(out=diff[c][:].rearrange(flat), in0=xs[:, :, 1], in1=xs[:, :, 0], op=ALU.subtract)
+            nc.vector.tensor_tensor(out=peak[c][:].rearrange(flat), in0=xs[:, :, 0], in1=xs[:, :, 1], op=ALU.max)
+            for j in range(PACK):
+                nc.vector.tensor_scalar(
+                    out=d_rows[c][:, j, :], in0=diff[c][:, j, :], scalar1=0.0, scalar2=fb_sb[:, j:j + 1],
+                    op0=ALU.max, op1=ALU.mult)
+                nc.vector.tensor_scalar(
+                    out=d_rows[c][:, PACK + j, :], in0=diff[c][:, j, :], scalar1=0.0, scalar2=fb_neg[:, j:j + 1],
+                    op0=ALU.min, op1=ALU.mult)
+
+        def scale_peaks(c):
+            for j in range(PACK):
+                nc.scalar.activation(out=u_rows[c][:, j, :], in_=peak[c][:, j, :], func=ACT.Copy, scale=fa_sb[:, j:j + 1])
+
+        def interleave_u(c, copy):
+            copy(
+                out=u_in[c][:].rearrange("p (h i j) -> p h j i", i=4, j=PACK),
+                in_=u_rows[c][:].rearrange("p j (h i) -> p h j i", i=4))
+
+        def interleave_d(c):
+            nc.scalar.copy(
+                out=d_in[c][:].rearrange("p (h i w) -> p h w i", i=4, w=2 * PACK),
+                in_=d_rows[c][:].rearrange("p w (h i) -> p h w i", i=4))
+
+        def quantize_inputs(c):
+            nc.vector.quantize_mx(out=d_codes[c][:].bitcast(FP8X4), scales=d_plane[c][:], in_=d_in[c][:])
+            nc.vector.quantize_mx(out=u_codes[c][:].bitcast(FP8X4), scales=u_plane[c][:], in_=u_in[c][:])
+
+        def deal_fp4(dealt, raw):
+            nc.vector.tensor_copy(
+                out=dealt[:].rearrange("p (z r m e) -> p z r m e", r=4, m=P, e=2),
+                in_=raw[:].rearrange("p (z m r e) -> p z r m e", r=4, m=P, e=2))
+
+        def deal_fp8(dealt, raw):
+            nc.vector.tensor_copy(
+                out=dealt[:].bitcast(I32).rearrange("p (r h i) -> p h r i", r=4, i=4),
+                in_=raw[:].bitcast(I32).rearrange("p (h i r) -> p h r i", r=4, i=4))
+
+        def deal_plane(dealt, raw):
+            nc.vector.tensor_copy(
+                out=dealt[:].rearrange("p (z r m) -> p z r m", r=4, m=P),
+                in_=raw[:].rearrange("p (z m r) -> p z r m", r=4, m=P))
+
+        zb = {}
+        za = {}
+
+        def open_zb(k):
+            zb[k] = zb_pool.tile([P, PACK, BLOCK], F32, name="zb")
+            h, t0 = divmod(k * BLOCK, HALF)
+            for z in range(PASSES_L):
+                for r in range(PACK):
+                    nc.tensor.matmul_mx(
+                        out=zb[k][:, r, :],
+                        lhsT=wq[:, 2 * (z * N + P * r):2 * (z * N + P * (r + 1))].bitcast(FP4X4),
+                        lhsT_scale=wq_plane[:, z * N + P * r:z * N + P * (r + 1)],
+                        rhs=xq[h][:, z, t0:t0 + BLOCK].bitcast(FP8X4),
+                        rhs_scale=xq_plane[:, z * T + k * BLOCK:z * T + (k + 1) * BLOCK],
+                        start=(z == 0 and r == 0), stop=False)
+
+        def close_zb(k):
+            c, t0 = divmod(k * BLOCK, CHUNK)
+            for r in range(PACK):
+                nc.tensor.matmul_mx(
+                    out=zb[k][:, r, :],
+                    lhsT=wb[:, 2 * P * r:2 * P * (r + 1)].bitcast(FP4X4),
+                    lhsT_scale=ab_plane[:, P * r:P * (r + 1)],
+                    rhs=d_codes[c][:, t0:t0 + BLOCK].bitcast(FP8X4),
+                    rhs_scale=d_plane[c][:, t0:t0 + BLOCK],
+                    start=False, stop=(r == PACK - 1))
+
+        def peak_product(c):
+            za[c] = za_pool.tile([P, PACK, PAIRS], F32, name="za")
+            for r in range(PACK):
+                nc.tensor.matmul_mx(
+                    out=za[c][:, r, :],
+                    lhsT=wa[:, P * r:P * (r + 1)].bitcast(FP8X4),
+                    lhsT_scale=ab_plane[4:P, P * r:P * (r + 1)],
+                    rhs=u_codes[c][:].bitcast(FP8X4),
+                    rhs_scale=u_plane[c][:],
+                    start=True, stop=True)
+
+        def relu_peaks(c):
+            nc.scalar.activation(out=ra[c][:], in_=za[c][:], func=ACT.Relu)
+
+        def add_up(k):
+            c, t0 = divmod(k * BLOCK, CHUNK)
+            b0 = t0 // 2
+            nc.vector.tensor_tensor(
+                out=y[c][:, :, t0:t0 + BLOCK].rearrange("p r (b s) -> p r b s", s=2),
+                in0=zb[k][:].rearrange("p r (b s) -> p r b s", s=2),
+                in1=ra[c][:, :, b0:b0 + BLOCK // 2].rearrange("p r (b o) -> p r b o", o=1).to_broadcast([P, PACK, BLOCK // 2, 2]),
+                op=ALU.add)
+
+        def store_y(t0, width):
+            c, o = divmod(t0, CHUNK)
+            nc.sync.dma_start(out=out_rows[:, :, t0:t0 + width], in_=y[c][:, :, o:o + width])
+
+        def round_y(k, copy):
+            c, t0 = divmod(k * BLOCK, CHUNK)
+            copy(
+                out=y_in[c][:, t0 * PACK:(t0 + BLOCK) * PACK].rearrange("p (h i r) -> p h r i", i=2, r=PACK),
+                in_=y[c][:, :, t0:t0 + BLOCK].rearrange("p r (h i) -> p h r i", i=2))
+
+        def quantize_y(t0, width):
+            c, o = divmod(t0, CHUNK)
+            cols = slice(t0, t0 + width)
+            nc.vector.quantize_mx(
+                out=y_codes[:, cols].bitcast(FP8X4), scales=y_plane[:, cols],
+                in_=y_in[c][:, o * PACK:(o + width) * PACK])
+
+        def store_codes(c):
+            cols = slice(c * CHUNK, (c + 1) * CHUNK)
+            nc.sync.dma_start(out=out_words[:, cols], in_=y_codes[:, cols].bitcast(I32))
+
+        last = CHUNKS - 1
+        deal_fp4(wq, wq_raw)
+        for c in range(CHUNKS):
+            pair_stats(c)
+            scale_peaks(c)
+            interleave_d(c)
+            if c < last:
+                interleave_u(c, nc.scalar.copy)
+            if c == 1:
+                deal_plane(wq_plane, wq_plane_raw)
+                for k in range(ZB_BANKS):
+                    open_zb(k)
+            if c == 2:
+                deal_fp4(wb, wb_raw)
+                deal_fp8(wa, wa_raw)
+        deal_plane(ab_plane, ab_plane_raw)
+        for c in range(last):
+            quantize_inputs(c)
+        interleave_u(last, nc.vector.tensor_copy)
+        quantize_inputs(last)
+
+        def products(c):
+            peak_product(c)
+            relu_peaks(c)
+            for k in (2 * c, 2 * c + 1):
+                if k not in zb:
+                    open_zb(k)
+                close_zb(k)
+
+        products(0)
+        products(1)
+        for c in range(last):
+            add_up(2 * c)
+            round_y(2 * c, nc.scalar.copy)
+            if c + 2 < CHUNKS:
+                products(c + 2)
+            add_up(2 * c + 1)
+            round_y(2 * c + 1, nc.scalar.copy)
+            store_y(c * CHUNK, CHUNK)
+            if c > 0:
+                quantize_y((c - 1) * CHUNK, CHUNK)
+                store_codes(c - 1)
+        add_up(2 * last)
+        store_y(last * CHUNK, BLOCK)
+        round_y(2 * last, nc.scalar.copy)
+        add_up(2 * last + 1)
+        store_y(last * CHUNK + BLOCK, BLOCK)
+        quantize_y((last - 1) * CHUNK, CHUNK)
+        store_codes(last - 1)
+        round_y(2 * last + 1, nc.vector.tensor_copy)
+        quantize_y(last * CHUNK, BLOCK)
+        quantize_y(last * CHUNK + BLOCK, BLOCK)
+        store_codes(last)
+        for q in range(4):
+            queue = nc.sync if q % 2 else nc.scalar
+            queue.dma_start(out=out_2[0, 4 * q:4 * q + 4, :].bitcast(I32), in_=y_plane[32 * q:32 * q + 4, :].bitcast(I32))

@@ -97,19 +97,21 @@ def tile_mix_group_peak_and_members_pl_kernel(
         nc.vector.memset(ab_plane_raw[:].bitcast(I32), 0)
         nc.gpsimd.memset(xq_plane[:].bitcast(I32), 0)
 
-        load_scales(nc.gpsimd, xq_plane, 0, xq_scales)
-        nc.sync.dma_start(out=wq_raw[:].bitcast(I32).rearrange("p (z c) -> p z c", z=PASSES_L), in_=wq_words.rearrange("z p c -> p z c").bitcast(I32))
+        nc.sync.dma_start(
+            out=wq_raw[:].bitcast(I32).rearrange("p (z c) -> p z c", z=PASSES_L),
+            in_=wq_words.rearrange("z p c -> p z c").bitcast(I32))
         load_x(0)
         nc.sync.dma_start(out=fa_sb[:], in_=fa.rearrange("(p j) o -> p (j o)", j=PACK))
         nc.sync.dma_start(out=fb_sb[:], in_=fb.rearrange("(p j) o -> p (j o)", j=PACK))
-        load_x(1)
         load_scales(nc.sync, wq_plane_raw, 0, wq_scales)
+        load_x(1)
+        load_scales(nc.sync, xq_plane, 0, xq_scales)
         load_xq(0)
         load_x(2)
         nc.sync.dma_start(out=wb_raw[:].bitcast(I32), in_=wb_words[0].bitcast(I32))
         nc.sync.dma_start(out=wa_raw[:].bitcast(I32), in_=wa_words[0].rearrange("p n r -> p (n r)").bitcast(I32))
-        load_x(3)
         load_scales(nc.sync, ab_plane_raw, 0, wb_scales)
+        load_x(3)
         load_scales(nc.sync, ab_plane_raw, 4, wa_scales)
         load_xq(1)
 
@@ -139,8 +141,8 @@ def tile_mix_group_peak_and_members_pl_kernel(
 
         def interleave_d(c):
             nc.scalar.copy(
-                out=d_in[c][:].rearrange("p (h i w) -> p h w i", i=4, w=2 * PACK),
-                in_=d_rows[c][:].rearrange("p w (h i) -> p h w i", i=4))
+                out=d_in[c][:].rearrange("p (h i w) -> p h w i", i=2, w=2 * PACK),
+                in_=d_rows[c][:].rearrange("p w (h i) -> p h w i", i=2))
 
         def quantize_inputs(c):
             nc.vector.quantize_mx(out=d_codes[c][:].bitcast(FP8X4), scales=d_plane[c][:], in_=d_in[c][:])
@@ -218,8 +220,8 @@ def tile_mix_group_peak_and_members_pl_kernel(
         def round_y(k, copy):
             c, t0 = divmod(k * BLOCK, CHUNK)
             copy(
-                out=y_in[c][:, t0 * PACK:(t0 + BLOCK) * PACK].rearrange("p (h i r) -> p h r i", i=2, r=PACK),
-                in_=y[c][:, :, t0:t0 + BLOCK].rearrange("p r (h i) -> p h r i", i=2))
+                out=y_in[c][:, t0 * PACK:(t0 + BLOCK) * PACK].rearrange("p (h i r) -> p h r i", i=4, r=PACK),
+                in_=y[c][:, :, t0:t0 + BLOCK].rearrange("p r (h i) -> p h r i", i=4))
 
         def quantize_y(t0, width):
             c, o = divmod(t0, CHUNK)
@@ -240,7 +242,7 @@ def tile_mix_group_peak_and_members_pl_kernel(
             interleave_d(c)
             if c < last:
                 interleave_u(c, nc.scalar.copy)
-            if c == 1:
+            if c == 0:
                 deal_plane(wq_plane, wq_plane_raw)
                 for k in range(ZB_BANKS):
                     open_zb(k)

@@ -44,7 +44,8 @@ def tile_mix_group_peak_and_members_pl_kernel(
         def one(name, shape, dtype):
             return sb.tile(shape, dtype, name=name, align_bytes=64)
 
-        x = tiles("x", CHUNKS, [P, PACK, CHUNK], F32)
+        x_first = tiles("x_first", 2, [P, PACK // 2, CHUNK], F32)
+        x = dict(zip(range(1, CHUNKS), tiles("x", CHUNKS - 1, [P, PACK, CHUNK], F32)))
         peak = tiles("peak", CHUNKS, [P, PACK, PAIRS], F32)
         diff = tiles("diff", CHUNKS, [P, PACK, PAIRS], F32)
         u_rows = tiles("u_rows", CHUNKS, [P, PACK, PAIRS], BF16)
@@ -97,31 +98,39 @@ def tile_mix_group_peak_and_members_pl_kernel(
         nc.vector.memset(ab_plane_raw[:].bitcast(I32), 0)
         nc.gpsimd.memset(xq_plane[:].bitcast(I32), 0)
 
+        nc.sync.dma_start(out=x_first[0][:], in_=xf_rows[:, 0:2, 0:CHUNK])
+        nc.sync.dma_start(out=fa_sb[:], in_=fa.rearrange("(p j) o -> p (j o)", j=PACK))
+        nc.sync.dma_start(out=x_first[1][:], in_=xf_rows[:, 2:4, 0:CHUNK])
+        nc.sync.dma_start(out=fb_sb[:], in_=fb.rearrange("(p j) o -> p (j o)", j=PACK))
+        load_x(1)
+        load_scales(nc.sync, wq_plane_raw, 0, wq_scales)
         nc.sync.dma_start(
             out=wq_raw[:].bitcast(I32).rearrange("p (z c) -> p z c", z=PASSES_L),
             in_=wq_words.rearrange("z p c -> p z c").bitcast(I32))
-        load_x(0)
-        nc.sync.dma_start(out=fa_sb[:], in_=fa.rearrange("(p j) o -> p (j o)", j=PACK))
-        nc.sync.dma_start(out=fb_sb[:], in_=fb.rearrange("(p j) o -> p (j o)", j=PACK))
-        load_scales(nc.sync, wq_plane_raw, 0, wq_scales)
-        load_x(1)
-        load_scales(nc.sync, xq_plane, 0, xq_scales)
-        load_xq(0)
         load_x(2)
-        nc.sync.dma_start(out=wb_raw[:].bitcast(I32), in_=wb_words[0].bitcast(I32))
+        load_scales(nc.sync, ab_plane_raw, 4, wa_scales)
+        load_xq(0)
+        load_scales(nc.sync, xq_plane, 0, xq_scales)
         nc.sync.dma_start(out=wa_raw[:].bitcast(I32), in_=wa_words[0].rearrange("p n r -> p (n r)").bitcast(I32))
+        nc.sync.dma_start(out=wb_raw[:].bitcast(I32), in_=wb_words[0].bitcast(I32))
         load_scales(nc.sync, ab_plane_raw, 0, wb_scales)
         load_x(3)
-        load_scales(nc.sync, ab_plane_raw, 4, wa_scales)
         load_xq(1)
 
         nc.scalar.activation(out=fb_neg[:], in_=fb_sb[:], func=ACT.Copy, scale=-1.0)
 
-        def pair_stats(c):
-            xs = x[c][:].rearrange("p j (b s) -> p (j b) s", s=2)
-            flat = "p j b -> p (j b)"
-            nc.vector.tensor_tensor(out=diff[c][:].rearrange(flat), in0=xs[:, :, 1], in1=xs[:, :, 0], op=ALU.subtract)
-            nc.vector.tensor_tensor(out=peak[c][:].rearrange(flat), in0=xs[:, :, 0], in1=xs[:, :, 1], op=ALU.max)
+        def pair_op(dst, src, first, op):
+            xs = src.rearrange("p j (b s) -> p (j b) s", s=2)
+            nc.vector.tensor_tensor(
+                out=dst.rearrange("p j b -> p (j b)"), in0=xs[:, :, first], in1=xs[:, :, 1 - first], op=op)
+
+        def pair_diff(c):
+            pair_op(diff[c][:], x[c][:], 1, ALU.subtract)
+
+        def pair_peak(c):
+            pair_op(peak[c][:], x[c][:], 0, ALU.max)
+
+        def distances(c):
             for j in range(PACK):
                 nc.vector.tensor_scalar(
                     out=d_rows[c][:, j, :], in0=diff[c][:, j, :], scalar1=0.0, scalar2=fb_sb[:, j:j + 1],
@@ -130,12 +139,12 @@ def tile_mix_group_peak_and_members_pl_kernel(
                     out=d_rows[c][:, PACK + j, :], in0=diff[c][:, j, :], scalar1=0.0, scalar2=fb_neg[:, j:j + 1],
                     op0=ALU.min, op1=ALU.mult)
 
-        def scale_peaks(c):
-            for j in range(PACK):
+        def scale_peaks(c, slots=range(PACK)):
+            for j in slots:
                 nc.scalar.activation(out=u_rows[c][:, j, :], in_=peak[c][:, j, :], func=ACT.Copy, scale=fa_sb[:, j:j + 1])
 
-        def interleave_u(c, copy):
-            copy(
+        def interleave_u(c):
+            nc.scalar.copy(
                 out=u_in[c][:].rearrange("p (h i j) -> p h j i", i=4, j=PACK),
                 in_=u_rows[c][:].rearrange("p j (h i) -> p h j i", i=4))
 
@@ -144,8 +153,10 @@ def tile_mix_group_peak_and_members_pl_kernel(
                 out=d_in[c][:].rearrange("p (h i w) -> p h w i", i=2, w=2 * PACK),
                 in_=d_rows[c][:].rearrange("p w (h i) -> p h w i", i=2))
 
-        def quantize_inputs(c):
+        def quantize_d(c):
             nc.vector.quantize_mx(out=d_codes[c][:].bitcast(FP8X4), scales=d_plane[c][:], in_=d_in[c][:])
+
+        def quantize_u(c):
             nc.vector.quantize_mx(out=u_codes[c][:].bitcast(FP8X4), scales=u_plane[c][:], in_=u_in[c][:])
 
         def deal_fp4(dealt, raw):
@@ -204,18 +215,18 @@ def tile_mix_group_peak_and_members_pl_kernel(
         def relu_peaks(c):
             nc.scalar.activation(out=ra[c][:], in_=za[c][:], func=ACT.Relu)
 
-        def add_up(k):
+        def add_up(k, rows=slice(0, PACK)):
             c, t0 = divmod(k * BLOCK, CHUNK)
             b0 = t0 // 2
+            shared = ra[c][:, rows, b0:b0 + BLOCK // 2].rearrange("p r (b o) -> p r b o", o=1)
             nc.vector.tensor_tensor(
-                out=y[c][:, :, t0:t0 + BLOCK].rearrange("p r (b s) -> p r b s", s=2),
-                in0=zb[k][:].rearrange("p r (b s) -> p r b s", s=2),
-                in1=ra[c][:, :, b0:b0 + BLOCK // 2].rearrange("p r (b o) -> p r b o", o=1).to_broadcast([P, PACK, BLOCK // 2, 2]),
+                out=y[c][:, rows, t0:t0 + BLOCK].rearrange("p r (b s) -> p r b s", s=2),
+                in0=zb[k][:, rows, :].rearrange("p r (b s) -> p r b s", s=2),
+                in1=shared.to_broadcast([P, rows.stop - rows.start, BLOCK // 2, 2]),
                 op=ALU.add)
 
-        def store_y(t0, width):
-            c, o = divmod(t0, CHUNK)
-            nc.sync.dma_start(out=out_rows[:, :, t0:t0 + width], in_=y[c][:, :, o:o + width])
+        def store_y(c, rows=slice(0, PACK)):
+            nc.sync.dma_start(out=out_rows[:, rows, c * CHUNK:(c + 1) * CHUNK], in_=y[c][:, rows, :])
 
         def round_y(k, copy):
             c, t0 = divmod(k * BLOCK, CHUNK)
@@ -223,70 +234,100 @@ def tile_mix_group_peak_and_members_pl_kernel(
                 out=y_in[c][:, t0 * PACK:(t0 + BLOCK) * PACK].rearrange("p (h i r) -> p h r i", i=4, r=PACK),
                 in_=y[c][:, :, t0:t0 + BLOCK].rearrange("p r (h i) -> p h r i", i=4))
 
-        def quantize_y(t0, width):
-            c, o = divmod(t0, CHUNK)
-            cols = slice(t0, t0 + width)
-            nc.vector.quantize_mx(
-                out=y_codes[:, cols].bitcast(FP8X4), scales=y_plane[:, cols],
-                in_=y_in[c][:, o * PACK:(o + width) * PACK])
-
-        def store_codes(c):
+        def quantize_y(c):
             cols = slice(c * CHUNK, (c + 1) * CHUNK)
+            nc.vector.quantize_mx(out=y_codes[:, cols].bitcast(FP8X4), scales=y_plane[:, cols], in_=y_in[c][:])
             nc.sync.dma_start(out=out_words[:, cols], in_=y_codes[:, cols].bitcast(I32))
 
-        last = CHUNKS - 1
-        deal_fp4(wq, wq_raw)
-        for c in range(CHUNKS):
-            pair_stats(c)
-            scale_peaks(c)
-            interleave_d(c)
-            if c < last:
-                interleave_u(c, nc.scalar.copy)
-            if c == 0:
-                deal_plane(wq_plane, wq_plane_raw)
-                for k in range(ZB_BANKS):
-                    open_zb(k)
-            if c == 2:
-                deal_fp4(wb, wb_raw)
-                deal_fp8(wa, wa_raw)
-        deal_plane(ab_plane, ab_plane_raw)
-        for c in range(last):
-            quantize_inputs(c)
-        interleave_u(last, nc.vector.tensor_copy)
-        quantize_inputs(last)
-
-        def products(c):
+        def peaks_out(c):
             peak_product(c)
             relu_peaks(c)
-            for k in (2 * c, 2 * c + 1):
-                if k not in zb:
-                    open_zb(k)
-                close_zb(k)
 
-        products(0)
-        products(1)
-        for c in range(last):
-            add_up(2 * c)
-            round_y(2 * c, nc.scalar.copy)
-            if c + 2 < CHUNKS:
-                products(c + 2)
-            add_up(2 * c + 1)
-            round_y(2 * c + 1, nc.scalar.copy)
-            store_y(c * CHUNK, CHUNK)
-            if c > 0:
-                quantize_y((c - 1) * CHUNK, CHUNK)
-                store_codes(c - 1)
-        add_up(2 * last)
-        store_y(last * CHUNK, BLOCK)
-        round_y(2 * last, nc.scalar.copy)
-        add_up(2 * last + 1)
-        store_y(last * CHUNK + BLOCK, BLOCK)
-        quantize_y((last - 1) * CHUNK, CHUNK)
-        store_codes(last - 1)
-        round_y(2 * last + 1, nc.vector.tensor_copy)
-        quantize_y(last * CHUNK, BLOCK)
-        quantize_y(last * CHUNK + BLOCK, BLOCK)
-        store_codes(last)
+        def close_chunk(c):
+            close_zb(2 * c)
+            close_zb(2 * c + 1)
+
+        def finish(k):
+            add_up(k)
+            round_y(k, nc.scalar.copy)
+
+        for half in range(2):
+            slots = slice(2 * half, 2 * half + 2)
+            pair_op(diff[0][:, slots, :], x_first[half][:], 1, ALU.subtract)
+            pair_op(peak[0][:, slots, :], x_first[half][:], 0, ALU.max)
+            scale_peaks(0, range(slots.start, slots.stop))
+        distances(0)
+        interleave_d(0)
+        interleave_u(0)
+        pair_diff(1)
+        pair_peak(1)
+        distances(1)
+        scale_peaks(1)
+        interleave_d(1)
+        interleave_u(1)
+
+        deal_fp4(wq, wq_raw)
+        pair_peak(2)
+        scale_peaks(2)
+        interleave_u(2)
+        deal_plane(wq_plane, wq_plane_raw)
+        for k in range(3):
+            open_zb(k)
+        pair_diff(2)
+        quantize_u(0)
+        distances(2)
+        interleave_d(2)
+        quantize_u(1)
+        deal_fp8(wa, wa_raw)
+        deal_plane(ab_plane, ab_plane_raw)
+        peaks_out(0)
+        peaks_out(1)
+        deal_fp4(wb, wb_raw)
+        quantize_u(2)
+        quantize_d(0)
+        close_chunk(0)
+        open_zb(3)
+        quantize_d(1)
+        pair_peak(3)
+        scale_peaks(3)
+        finish(0)
+        interleave_u(3)
+        peaks_out(2)
+        close_chunk(1)
+        open_zb(4)
+        open_zb(5)
+        finish(1)
+        store_y(0)
+        pair_diff(3)
+        quantize_d(2)
+        close_chunk(2)
+        distances(3)
+        interleave_d(3)
+        quantize_u(3)
+        peaks_out(3)
+        open_zb(6)
+        open_zb(7)
+        finish(2)
+        finish(3)
+        store_y(1)
+        quantize_y(0)
+        finish(4)
+        quantize_d(3)
+        close_chunk(3)
+        finish(5)
+        store_y(2)
+        low, high = slice(0, 2), slice(2, 4)
+        add_up(6, low)
+        add_up(7, low)
+        store_y(3, low)
+        quantize_y(1)
+        add_up(6, high)
+        round_y(6, nc.scalar.copy)
+        add_up(7, high)
+        store_y(3, high)
+        round_y(7, nc.vector.tensor_copy)
+        quantize_y(2)
+        quantize_y(3)
         for q in range(4):
             queue = nc.sync if q % 2 else nc.scalar
             queue.dma_start(out=out_2[0, 4 * q:4 * q + 4, :].bitcast(I32), in_=y_plane[32 * q:32 * q + 4, :].bitcast(I32))

from contextlib import ExitStack

import concourse.mybir as mybir

K, L, T, B, N = 512, 1024, 1024, 512, 512
FLOPS = 2 * N * (K * B + K * T + L * T)

F32 = mybir.dt.float32
BF16 = mybir.dt.bfloat16
I32 = mybir.dt.int32
U32 = mybir.dt.uint32
U8 = mybir.dt.uint8
FP8X4 = mybir.dt.float8_e4m3fn_x4
FP4X4 = mybir.dt.float4_e2m1fn_x4
ALU = mybir.AluOpType
ACT = mybir.ActivationFunctionType

P = 128
PACK = 4
PASSES_L = L // (P * PACK)
CHUNK = 256
PAIRS = CHUNK // 2
CHUNKS = T // CHUNK
BLOCK = 128
HALF = 512
ZB_BANKS = 6
ZA_BANKS = 2


def tile_mix_group_peak_and_members_pl_kernel(
    tc, xf, fa, fb, wa_words, wa_scales, wb_words, wb_scales, xq_words, xq_scales, wq_words, wq_scales,
    out_0, out_1, out_2,
):
    nc = tc.nc
    with ExitStack() as ctx:
        sb = ctx.enter_context(tc.tile_pool(name="sb", bufs=1))
        zb_pool = ctx.enter_context(tc.psum_pool(name="zb", bufs=ZB_BANKS))
        za_pool = ctx.enter_context(tc.psum_pool(name="za", bufs=ZA_BANKS))
        ctx.enter_context(tc.manual_schedule())

        def tiles(name, count, shape, dtype):
            return [sb.tile(shape, dtype, name="%s%d" % (name, i), align_bytes=64) for i in range(count)]

        def one(name, shape, dtype):
            return sb.tile(shape, dtype, name=name, align_bytes=64)

        x_first = tiles("x_first", 2, [P, PACK // 2, CHUNK], F32)
        x = dict(zip(range(1, CHUNKS), tiles("x", CHUNKS - 1, [P, PACK, CHUNK], F32)))
        peak = tiles("peak", CHUNKS, [P, PACK, PAIRS], F32)
        diff = tiles("diff", CHUNKS, [P, PACK, PAIRS], F32)
        u_rows = tiles("u_rows", CHUNKS, [P, PACK, PAIRS], BF16)
        d_rows = tiles("d_rows", CHUNKS, [P, 2 * PACK, PAIRS], BF16)
        u_in = tiles("u_in", CHUNKS, [P, PAIRS * PACK], BF16)
        d_in = tiles("d_in", CHUNKS, [P, CHUNK * PACK], BF16)
        u_codes = tiles("u_codes", CHUNKS, [P, PAIRS], U32)
        u_plane = tiles("u_plane", CHUNKS, [P, PAIRS], U8)
        d_codes = tiles("d_codes", CHUNKS, [P, CHUNK], U32)
        d_plane = tiles("d_plane", CHUNKS, [P, CHUNK], U8)
        ra = tiles("ra", CHUNKS, [P, PACK, PAIRS], F32)
        y = tiles("y", CHUNKS, [P, PACK, CHUNK], F32)
        y_in = tiles("y_in", CHUNKS, [P, CHUNK * PACK], BF16)
        xq = tiles("xq", T // HALF, [P, PASSES_L, HALF], U32)
        fa_sb = one("fa_sb", [P, PACK], F32)
        fb_sb = one("fb_sb", [P, PACK], F32)
        fb_neg = one("fb_neg", [P, PACK], F32)
        wa_raw = one("wa_raw", [P, N], U32)
        wa = one("wa", [P, N], U32)
        wb_raw = one("wb_raw", [P, 2 * N], U8)
        wb = one("wb", [P, 2 * N], U8)
        wq_raw = one("wq_raw", [P, PASSES_L * 2 * N], U8)
        wq = one("wq", [P, PASSES_L * 2 * N], U8)
        ab_plane_raw = one("ab_plane_raw", [P, N], U8)
        ab_plane = one("ab_plane", [P, N], U8)
        wq_plane_raw = one("wq_plane_raw", [P, PASSES_L * N], U8)
        wq_plane = one("wq_plane", [P, PASSES_L * N], U8)
        xq_plane = one("xq_plane", [P, PASSES_L * T], U8)
        y_codes = one("y_codes", [P, T], U32)
        y_plane = one("y_plane", [P, T], U8)

        xf_rows = xf.rearrange("(p j) t -> p j t", j=PACK)
        out_rows = out_0.rearrange("(p r) t -> p r t", r=PACK)
        out_words = out_1[0].rearrange("p t r -> p (t r)").bitcast(I32)

        def load_x(c):
            nc.sync.dma_start(out=x[c][:], in_=xf_rows[:, :, c * CHUNK:(c + 1) * CHUNK])

        def load_xq(h):
            src = xq_words.rearrange("z p t r -> p z (t r)")[:, :, h * HALF * 4:(h + 1) * HALF * 4]
            nc.sync.dma_start(out=xq[h][:].bitcast(I32), in_=src.bitcast(I32))

        def load_scales(queue, plane, first, scales):
            rows = scales.bitcast(I32).rearrange("z (q r) c -> r q z c", r=4)
            words = plane[:].bitcast(I32).rearrange("p (z c) -> p z c", z=scales.shape[0])
            for r in range(4):
                queue.dma_start(out=words[first + r:P:32, :, :], in_=rows[r])

        nc.vector.memset(wq_plane_raw[:].bitcast(I32), 0)
        nc.vector.memset(ab_plane_raw[:].bitcast(I32), 0)
        nc.gpsimd.memset(xq_plane[:].bitcast(I32), 0)

        nc.sync.dma_start(out=x_first[0][:], in_=xf_rows[:, 0:2, 0:CHUNK])
        nc.sync.dma_start(out=fa_sb[:], in_=fa.rearrange("(p j) o -> p (j o)", j=PACK))
        nc.sync.dma_start(out=x_first[1][:], in_=xf_rows[:, 2:4, 0:CHUNK])
        nc.sync.dma_start(out=fb_sb[:], in_=fb.rearrange("(p j) o -> p (j o)", j=PACK))
        load_x(1)
        load_scales(nc.sync, wq_plane_raw, 0, wq_scales)
        nc.sync.dma_start(
            out=wq_raw[:].bitcast(I32).rearrange("p (z c) -> p z c", z=PASSES_L),
            in_=wq_words.rearrange("z p c -> p z c").bitcast(I32))
        load_x(2)
        load_scales(nc.sync, ab_plane_raw, 4, wa_scales)
        load_xq(0)
        load_scales(nc.sync, xq_plane, 0, xq_scales)
        nc.sync.dma_start(out=wa_raw[:].bitcast(I32), in_=wa_words[0].rearrange("p n r -> p (n r)").bitcast(I32))
        nc.sync.dma_start(out=wb_raw[:].bitcast(I32), in_=wb_words[0].bitcast(I32))
        load_scales(nc.sync, ab_plane_raw, 0, wb_scales)
        load_x(3)
        load_xq(1)

        nc.scalar.activation(out=fb_neg[:], in_=fb_sb[:], func=ACT.Copy, scale=-1.0)

        def pair_op(dst, src, first, op):
            xs = src.rearrange("p j (b s) -> p (j b) s", s=2)
            nc.vector.tensor_tensor(
                out=dst.rearrange("p j b -> p (j b)"), in0=xs[:, :, first], in1=xs[:, :, 1 - first], op=op)

        def pair_diff(c):
            pair_op(diff[c][:], x[c][:], 1, ALU.subtract)

        def pair_peak(c):
            pair_op(peak[c][:], x[c][:], 0, ALU.max)

        def distances(c):
            for j in range(PACK):
                nc.vector.tensor_scalar(
                    out=d_rows[c][:, j, :], in0=diff[c][:, j, :], scalar1=0.0, scalar2=fb_sb[:, j:j + 1],
                    op0=ALU.max, op1=ALU.mult)
                nc.vector.tensor_scalar(
                    out=d_rows[c][:, PACK + j, :], in0=diff[c][:, j, :], scalar1=0.0, scalar2=fb_neg[:, j:j + 1],
                    op0=ALU.min, op1=ALU.mult)

        def scale_peaks(c, slots=range(PACK)):
            for j in slots:
                nc.scalar.activation(out=u_rows[c][:, j, :], in_=peak[c][:, j, :], func=ACT.Copy, scale=fa_sb[:, j:j + 1])

        def interleave_u(c):
            nc.scalar.copy(
                out=u_in[c][:].rearrange("p (h i j) -> p h j i", i=4, j=PACK),
                in_=u_rows[c][:].rearrange("p j (h i) -> p h j i", i=4))

        def interleave_d(c):
            nc.scalar.copy(
                out=d_in[c][:].rearrange("p (h i w) -> p h w i", i=2, w=2 * PACK),
                in_=d_rows[c][:].rearrange("p w (h i) -> p h w i", i=2))

        def quantize_d(c):
            nc.vector.quantize_mx(out=d_codes[c][:].bitcast(FP8X4), scales=d_plane[c][:], in_=d_in[c][:])

        def quantize_u(c):
            nc.vector.quantize_mx(out=u_codes[c][:].bitcast(FP8X4), scales=u_plane[c][:], in_=u_in[c][:])

        def deal_fp4(dealt, raw):
            nc.vector.tensor_copy(
                out=dealt[:].rearrange("p (z r m e) -> p z r m e", r=4, m=P, e=2),
                in_=raw[:].rearrange("p (z m r e) -> p z r m e", r=4, m=P, e=2))

        def deal_fp8(dealt, raw):
            nc.vector.tensor_copy(
                out=dealt[:].bitcast(I32).rearrange("p (r h i) -> p h r i", r=4, i=4),
                in_=raw[:].bitcast(I32).rearrange("p (h i r) -> p h r i", r=4, i=4))

        def deal_plane(dealt, raw):
            nc.vector.tensor_copy(
                out=dealt[:].rearrange("p (z r m) -> p z r m", r=4, m=P),
                in_=raw[:].rearrange("p (z m r) -> p z r m", r=4, m=P))

        zb = {}
        za = {}

        def open_zb(k):
            zb[k] = zb_pool.tile([P, PACK, BLOCK], F32, name="zb")
            h, t0 = divmod(k * BLOCK, HALF)
            for z in range(PASSES_L):
                for r in range(PACK):
                    nc.tensor.matmul_mx(
                        out=zb[k][:, r, :],
                        lhsT=wq[:, 2 * (z * N + P * r):2 * (z * N + P * (r + 1))].bitcast(FP4X4),
                        lhsT_scale=wq_plane[:, z * N + P * r:z * N + P * (r + 1)],
                        rhs=xq[h][:, z, t0:t0 + BLOCK].bitcast(FP8X4),
                        rhs_scale=xq_plane[:, z * T + k * BLOCK:z * T + (k + 1) * BLOCK],
                        start=(z == 0 and r == 0), stop=False)

        def close_zb(k):
            c, t0 = divmod(k * BLOCK, CHUNK)
            for r in range(PACK):
                nc.tensor.matmul_mx(
                    out=zb[k][:, r, :],
                    lhsT=wb[:, 2 * P * r:2 * P * (r + 1)].bitcast(FP4X4),
                    lhsT_scale=ab_plane[:, P * r:P * (r + 1)],
                    rhs=d_codes[c][:, t0:t0 + BLOCK].bitcast(FP8X4),
                    rhs_scale=d_plane[c][:, t0:t0 + BLOCK],
                    start=False, stop=(r == PACK - 1))

        def peak_product(c):
            za[c] = za_pool.tile([P, PACK, PAIRS], F32, name="za")
            for r in range(PACK):
                nc.tensor.matmul_mx(
                    out=za[c][:, r, :],
                    lhsT=wa[:, P * r:P * (r + 1)].bitcast(FP8X4),
                    lhsT_scale=ab_plane[4:P, P * r:P * (r + 1)],
                    rhs=u_codes[c][:].bitcast(FP8X4),
                    rhs_scale=u_plane[c][:],
                    start=True, stop=True)

        def relu_peaks(c):
            nc.scalar.activation(out=ra[c][:], in_=za[c][:], func=ACT.Relu)

        def add_up(k, rows=slice(0, PACK)):
            c, t0 = divmod(k * BLOCK, CHUNK)
            b0 = t0 // 2
            shared = ra[c][:, rows, b0:b0 + BLOCK // 2].rearrange("p r (b o) -> p r b o", o=1)
            nc.vector.tensor_tensor(
                out=y[c][:, rows, t0:t0 + BLOCK].rearrange("p r (b s) -> p r b s", s=2),
                in0=zb[k][:, rows, :].rearrange("p r (b s) -> p r b s", s=2),
                in1=shared.to_broadcast([P, rows.stop - rows.start, BLOCK // 2, 2]),
                op=ALU.add)

        def store_y(c, rows=slice(0, PACK)):
            nc.sync.dma_start(out=out_rows[:, rows, c * CHUNK:(c + 1) * CHUNK], in_=y[c][:, rows, :])

        def round_y(k, copy):
            c, t0 = divmod(k * BLOCK, CHUNK)
            copy(
                out=y_in[c][:, t0 * PACK:(t0 + BLOCK) * PACK].rearrange("p (h i r) -> p h r i", i=4, r=PACK),
                in_=y[c][:, :, t0:t0 + BLOCK].rearrange("p r (h i) -> p h r i", i=4))

        def quantize_y(c):
            cols = slice(c * CHUNK, (c + 1) * CHUNK)
            nc.vector.quantize_mx(out=y_codes[:, cols].bitcast(FP8X4), scales=y_plane[:, cols], in_=y_in[c][:])
            nc.sync.dma_start(out=out_words[:, cols], in_=y_codes[:, cols].bitcast(I32))

        def peaks_out(c):
            peak_product(c)
            relu_peaks(c)

        def close_chunk(c):
            close_zb(2 * c)
            close_zb(2 * c + 1)

        def finish(k):
            add_up(k)
            round_y(k, nc.scalar.copy)

        for half in range(2):
            slots = slice(2 * half, 2 * half + 2)
            pair_op(diff[0][:, slots, :], x_first[half][:], 1, ALU.subtract)
            pair_op(peak[0][:, slots, :], x_first[half][:], 0, ALU.max)
            scale_peaks(0, range(slots.start, slots.stop))
        distances(0)
        interleave_d(0)
        interleave_u(0)
        pair_diff(1)
        pair_peak(1)
        distances(1)
        scale_peaks(1)
        interleave_d(1)
        interleave_u(1)

        deal_fp4(wq, wq_raw)
        pair_peak(2)
        scale_peaks(2)
        interleave_u(2)
        deal_plane(wq_plane, wq_plane_raw)
        for k in range(3):
            open_zb(k)
        pair_diff(2)
        quantize_u(0)
        distances(2)
        interleave_d(2)
        quantize_u(1)
        deal_fp8(wa, wa_raw)
        deal_plane(ab_plane, ab_plane_raw)
        peaks_out(0)
        peaks_out(1)
        deal_fp4(wb, wb_raw)
        quantize_u(2)
        quantize_d(0)
        close_chunk(0)
        open_zb(3)
        quantize_d(1)
        pair_peak(3)
        scale_peaks(3)
        finish(0)
        interleave_u(3)
        peaks_out(2)
        close_chunk(1)
        open_zb(4)
        open_zb(5)
        finish(1)
        store_y(0)
        pair_diff(3)
        quantize_d(2)
        close_chunk(2)
        distances(3)
        interleave_d(3)
        quantize_u(3)
        peaks_out(3)
        open_zb(6)
        open_zb(7)
        finish(2)
        finish(3)
        store_y(1)
        quantize_y(0)
        finish(4)
        quantize_d(3)
        close_chunk(3)
        finish(5)
        store_y(2)
        low, high = slice(0, 2), slice(2, 4)
        add_up(6, low)
        add_up(7, low)
        store_y(3, low)
        quantize_y(1)
        add_up(6, high)
        round_y(6, nc.scalar.copy)
        add_up(7, high)
        store_y(3, high)
        round_y(7, nc.vector.tensor_copy)
        quantize_y(2)
        quantize_y(3)
        for q in range(4):
            queue = nc.sync if q % 2 else nc.scalar
            queue.dma_start(out=out_2[0, 4 * q:4 * q + 4, :].bitcast(I32), in_=y_plane[32 * q:32 * q + 4, :].bitcast(I32))
